import numpy as np
import ml_dtypes


def mxq(x, axis, fmt="e4m3"):
    dtype, down = {"e4m3": (ml_dtypes.float8_e4m3fn, 7), "e5m2": (ml_dtypes.float8_e5m2, 14)}[fmt]
    v = np.moveaxis(np.asarray(x, np.float32).astype(ml_dtypes.bfloat16).astype(np.float64), axis, -1)
    blocks = v.reshape(v.shape[:-1] + (-1, 32))
    amax = np.abs(blocks).max(-1, keepdims=True)
    byte = np.maximum(np.where(amax > 0, np.frexp(amax)[1] - 1 + 127, 0) - down, 1)
    scale = np.exp2(byte - 127.0)
    codes = (blocks / scale).astype(np.float32).astype(dtype).astype(np.float64)
    return np.moveaxis((codes * scale).reshape(v.shape), -1, axis)


WIDE = False


def mx_kscale(k):
    if not WIDE:
        return np.ones(k)
    levels = np.array([10, -10, 5, -5, 0])
    if k % 512:
        return np.exp2(np.random.permutation(np.resize(levels, k // 32))).repeat(32)
    a = np.empty((k // 512, 16))
    for p in range(k // 512):
        a[p, :8] = np.random.permutation(np.resize(levels, 8))
        for g in range(8):
            far = levels[np.abs(levels - a[p, g]) >= 10]
            a[p, g + 8] = far[np.random.randint(len(far))]
    return np.exp2(a.ravel()).repeat(32)


def f64(x):
    return np.asarray(x).astype(np.float64)


def striped(idx):
    return np.tile(idx.reshape(-1, 16).T, (8, 1)).astype(np.uint16)


def unstriped(offs):
    return offs[:16].T.reshape(-1).astype(np.int64)


E2M1 = np.array([0.0, 0.5, 1.0, 1.5, 2.0, 3.0, 4.0, 6.0, -0.0, -0.5, -1.0, -1.5, -2.0, -3.0, -4.0, -6.0])


def pack_weight(w, fmt):
    k, n = w.shape
    w = f64(np.asarray(w, np.float32).astype(ml_dtypes.bfloat16)).reshape(k // 32, 32, n)
    amax = np.abs(w).max(1)
    if fmt == "e4m3":
        byte = np.frexp(amax)[1] - 1 + 127 - 7
    else:
        mant, ex = np.frexp(amax / 6.0)
        byte = np.where(mant > 0.5, ex, ex - 1) + 127
    byte = np.clip(np.where(amax > 0, byte, 1), 1, 254)
    scaled = (w * np.exp2(127.0 - byte)[:, None, :]).reshape(k, n).astype(np.float32)
    by_word = np.ascontiguousarray(scaled.reshape(k // 512, 128, 4, n).transpose(0, 1, 3, 2))
    if fmt == "e4m3":
        words = by_word.astype(ml_dtypes.float8_e4m3fn).view(np.uint8)
    else:
        c = by_word.astype(ml_dtypes.float4_e2m1fn).view(np.uint8) & 0xF
        words = (c[..., 0::2] | (c[..., 1::2] << 4)).reshape(k // 512, 128, 2 * n)
    return np.ascontiguousarray(words), np.ascontiguousarray(byte.astype(np.uint8).reshape(k // 512, 16, n))


def unpack_weight(words, scales, fmt):
    g, _, n = scales.shape
    words = np.ascontiguousarray(words).reshape(g, 128, n, -1)
    if fmt == "e4m3":
        vals = words.view(ml_dtypes.float8_e4m3fn).astype(np.float64)
    else:
        nib = np.empty((g, 128, n, 4), np.uint8)
        nib[..., 0::2] = words & 0xF
        nib[..., 1::2] = words >> 4
        vals = E2M1[nib]
    vals = vals * np.repeat(np.exp2(scales.astype(np.float64) - 127.0), 8, axis=1)[..., None]
    return vals.transpose(0, 1, 3, 2).reshape(g * 512, n)


def planes(y):
    n, m = y.shape
    v = y.astype(np.float32).astype(ml_dtypes.bfloat16).astype(np.float64).reshape(n // 32, 32, m)
    top = np.abs(v).max(1)
    byte = np.clip(np.where(top > 0, np.frexp(top)[1] - 1 + 127 - 7, 1), 1, 254)
    codes = (v * np.exp2(127.0 - byte)[:, None, :]).reshape(n, m).astype(np.float32).astype(ml_dtypes.float8_e4m3fn).view(np.uint8)
    words = codes.reshape(n // 512, 128, 4, m).transpose(0, 1, 3, 2)
    return np.ascontiguousarray(words), np.ascontiguousarray(byte.astype(np.uint8).reshape(n // 512, 16, m))


def silu(v):
    return v / (1.0 + np.exp(-np.maximum(v, -700.0)))


K, T, G, C1, E, C2, H = 512, 768, 3, 256, 6, 128, 512
N = 512


def by_expert(wq, xq, E, C):
    return np.concatenate([wq[e].T @ xq[:, e * C:(e + 1) * C] for e in range(E)], axis=1)


def setup_inputs():
    n = np.random.standard_normal
    s = mx_kscale(K)
    u = mx_kscale(H)
    slots1 = np.random.permutation(T)
    slots2 = np.concatenate([q * C1 + np.random.permutation(C1) for q in range(G)])
    x = pack_weight(n((K, T)) * s[:, None], "e4m3")
    wg = [pack_weight(m, "e2m1") for m in n((G, K, H)) / np.sqrt(K) / s[None, :, None] * u]
    we = [pack_weight(m, "e4m3") for m in n((E, H, N)) / np.sqrt(H) / u[None, :, None]]
    return {
        "x_words": x[0],
        "x_scales": x[1],
        "wg_words": np.stack([m[0] for m in wg]),
        "wg_scales": np.stack([m[1] for m in wg]),
        "we_words": np.stack([m[0] for m in we]),
        "we_scales": np.stack([m[1] for m in we]),
        "gate": (np.tile(np.random.uniform(0.2, 1.0, T), (128, 1))).astype(np.float32),
        "offs": striped(slots1),
        "offs2": striped(slots2),
        "dst": striped(slots1[slots2]),
    }


def reference(x_words, x_scales, wg_words, wg_scales, we_words, we_scales, gate, offs, offs2, dst):
    wg = np.stack([unpack_weight(wg_words[e], wg_scales[e], "e2m1") for e in range(G)])
    we = np.stack([unpack_weight(we_words[e], we_scales[e], "e4m3") for e in range(E)])
    idx, idx2 = unstriped(offs), unstriped(offs2)
    xq = unpack_weight(x_words, x_scales, "e4m3")[:, idx]
    a = silu(by_expert(wg, xq, G, C1))
    y = by_expert(we, mxq(a[:, idx2], 0, "e4m3"), E, C2)
    out = np.zeros((N, T))
    out[:, unstriped(dst)] = f64(gate[:1]) * y
    out_0 = out
    return (out_0,) + planes(out_0)

@@ -1,0 +1,204 @@
+from contextlib import ExitStack
+
+import concourse.mybir as mybir
+from concourse.masks import make_identity
+
+K, T, G, C1, E, C2, H, N = 512, 768, 3, 256, 6, 128, 512, 512
+FLOPS = 2 * T * K * H + 2 * T * H * N
+
+F32 = mybir.dt.float32
+BF16 = mybir.dt.bfloat16
+I32 = mybir.dt.int32
+U32 = mybir.dt.uint32
+U16 = mybir.dt.uint16
+U8 = mybir.dt.uint8
+FP8X4 = mybir.dt.float8_e4m3fn_x4
+FP4X4 = mybir.dt.float4_e2m1fn_x4
+ACT = mybir.ActivationFunctionType
+
+P = 128
+PACK = 4
+LIST = 16
+MIN_WINDOW = 512
+PAIR_BASE = (0, 3 * C1, 5 * C1)
+EARLY = 3
+
+
+def load_scale_rows(queue, plane, rows):
+    for r in range(4):
+        queue.dma_start(out=plane[r:P:32].bitcast(I32), in_=rows[r:16:4].bitcast(I32))
+
+
+def tile_moe_hie_silu_kernel(
+    tc, x_words, x_scales, wg_words, wg_scales, we_words, we_scales, gate, offs, offs2, dst, out_0, out_1, out_2
+):
+    nc = tc.nc
+    with ExitStack() as ctx:
+        keep = ctx.enter_context(tc.tile_pool(name="keep", bufs=1))
+        ring = ctx.enter_context(tc.tile_pool(name="ring", bufs=3))
+        psum = ctx.enter_context(tc.psum_pool(name="psum", bufs=2))
+
+        offs_sb = keep.tile([P, T // LIST], U16, name="offs_sb")
+        offs2_sb = keep.tile([P, T // LIST], U16, name="offs2_sb")
+        dst_sb = keep.tile([P, T // LIST], U16, name="dst_sb")
+        x_sb = keep.tile([P, T], I32, name="x_sb", align_bytes=64)
+        xs_sb = keep.tile([P, T], U8, name="xs_sb", align_bytes=64)
+        wgs_sb = keep.tile([P, G, H], U8, name="wgs_sb", align_bytes=64)
+        wes_sb = keep.tile([P, E, N], U8, name="wes_sb", align_bytes=64)
+        wg_sb = [keep.tile([P, 2 * H], U8, name="wg_sb%d" % f, align_bytes=64) for f in range(G)]
+        we_sb = [keep.tile([P, N], I32, name="we_sb%d" % e, align_bytes=64) for e in range(E)]
+        gate_col = keep.tile([P, E], F32, name="gate_col")
+        ident = keep.tile([P, P], F32, name="ident")
+        pairs = keep.tile([P, 7 * C1], F32, name="pairs", align_bytes=64)
+        y_sb = keep.tile([P, PACK, T], F32, name="y_sb", align_bytes=64)
+        out_sb = [keep.tile([P, T], F32, name="out_sb%d" % t, align_bytes=64) for t in range(PACK)]
+        out_bf = keep.tile([P, T * PACK], BF16, name="out_bf", align_bytes=64)
+        out_codes = keep.tile([P, T], I32, name="out_codes", align_bytes=64)
+        out_scales = keep.tile([P, T], U8, name="out_scales", align_bytes=64)
+
+        nc.gpsimd.memset(xs_sb[:].bitcast(I32), 0)
+        nc.gpsimd.memset(wgs_sb[:].bitcast(I32), 0)
+        make_identity(nc, ident[:])
+        nc.vector.memset(wes_sb[:].bitcast(I32), 0)
+        nc.scalar.activation(
+            out=pairs[:, 2 * C1 : 3 * C1].rearrange("p (a b) -> p a b", a=2),
+            in_=ident[:].unsqueeze(1).to_broadcast([P, 2, P]),
+            func=ACT.Silu,
+            scale=0.0,
+        )
+
+        def words_of(ap):
+            return ap.rearrange("p n d -> p (n d)").bitcast(I32)
+
+        nc.sync.dma_start(out=x_sb[:], in_=words_of(x_words[0]))
+        nc.sync.dma_start(offs_sb[:], offs)
+        load_scale_rows(nc.scalar, xs_sb, x_scales[0])
+        nc.sync.dma_start(out=wg_sb[0][:].bitcast(I32), in_=wg_words[0, 0].bitcast(I32))
+        load_scale_rows(nc.sync, wgs_sb, wg_scales.rearrange("f s b i -> b (f s) i"))
+        nc.sync.dma_start(out=wg_sb[1][:].bitcast(I32), in_=wg_words[1, 0].bitcast(I32))
+        nc.sync.dma_start(offs2_sb[:], offs2)
+        nc.sync.dma_start(out=wg_sb[2][:].bitcast(I32), in_=wg_words[2, 0].bitcast(I32))
+        nc.sync.dma_start(out=we_sb[0][:], in_=words_of(we_words[0, 0]))
+        load_scale_rows(nc.sync, wes_sb, we_scales.rearrange("e s b n -> b (e s) n"))
+        with nc.allow_non_contiguous_dma(reason="one gate value a partition and expert"):
+            nc.sync.dma_start(out=gate_col[:], in_=gate[0].rearrange("(e m) -> m e", m=C2))
+        nc.sync.dma_start(dst_sb[:], dst)
+        for e in range(1, E):
+            nc.sync.dma_start(out=we_sb[e][:], in_=words_of(we_words[e, 0]))
+
+        def entries(lst, lo, hi):
+            return lst[:, lo // LIST : hi // LIST]
+
+        def first_level(f, cuts):
+            xg = keep.tile([P, C1], I32, name="xg%d" % f, align_bytes=64)
+            xgs = keep.tile([P, C1], U8, name="xgs%d" % f, align_bytes=64)
+            for lo, hi in cuts:
+                slots = entries(offs_sb, f * C1 + lo, f * C1 + hi)
+                nc.vector.tensor_copy(xg[:, lo:hi].bitcast(U32), x_sb[:].bitcast(U32).indirect(slots))
+                nc.vector.tensor_copy(xgs[:, lo:hi], xs_sb[:].indirect(slots))
+            turned = psum.tile([P, 2, C1], F32, name="a_turned")
+            for h in range(C1 // P):
+                cols = slice(h * P, (h + 1) * P)
+                acc = psum.tile([P, H], F32, name="a_acc")
+                nc.tensor.matmul_mx(
+                    out=acc[:],
+                    lhsT=xg[:, cols].bitcast(FP8X4),
+                    lhsT_scale=xgs[:, cols],
+                    rhs=wg_sb[f][:].bitcast(FP4X4),
+                    rhs_scale=wgs_sb[:, f, :],
+                    start=True,
+                    stop=True,
+                )
+                a_rows = ring.tile([P, H], BF16, name="a_rows", align_bytes=64)
+                nc.scalar.activation(
+                    out=a_rows[:].rearrange("s (u p d) -> s u p d", u=2, d=2),
+                    in_=acc[:].rearrange("s (p u d) -> s u p d", u=2, d=2),
+                    func=ACT.Silu,
+                )
+                a_words = a_rows[:].bitcast(F32)
+                for u in range(2):
+                    nc.tensor.transpose(turned[:, u, cols], a_words[:, u * P : (u + 1) * P], ident[:])
+            base = PAIR_BASE[f]
+            nc.scalar.copy(out=pairs[:, base : base + 2 * C1], in_=turned[:].rearrange("p u s -> p (u s)"))
+
+        def second_level(e):
+            f = e // 2
+            slots = entries(offs2_sb, e * C2, (e + 1) * C2)
+            ag = ring.tile([P, C2 * PACK], BF16, name="ag", align_bytes=64)
+            ag_words = ag[:].bitcast(U32).rearrange("p (s u) -> p s u", u=2)
+            ag_halves = ring.tile([P, 2, C2], I32, name="ag_halves", align_bytes=64)
+            width = max(MIN_WINDOW, (f + 1) * C1)
+            for u in range(2):
+                start = PAIR_BASE[f] + (u - f) * C1
+                window = pairs[:, start : start + width].bitcast(U32)
+                target = ag_words[:, :, u] if e == 0 else ag_halves[:, u, :].bitcast(U32)
+                nc.vector.tensor_copy(target, window.indirect(slots))
+            if e > 0:
+                nc.scalar.copy(out=ag_words, in_=ag_halves[:].bitcast(U32).rearrange("p u s -> p s u"))
+            aq = ring.tile([P, C2], I32, name="aq", align_bytes=64)
+            aqs = ring.tile([P, C2], U8, name="aqs", align_bytes=64)
+            nc.vector.quantize_mx(out=aq[:].bitcast(FP8X4), scales=aqs[:], in_=ag[:])
+            acc = psum.tile([P, N], F32, name="y_acc")
+            nc.tensor.matmul_mx(
+                out=acc[:],
+                lhsT=aq[:].bitcast(FP8X4),
+                lhsT_scale=aqs[:],
+                rhs=we_sb[e][:].bitcast(FP8X4),
+                rhs_scale=wes_sb[:, e, :],
+                start=True,
+                stop=True,
+            )
+            y_rows = ring.tile([P, PACK, P], F32, name="y_rows", align_bytes=64)
+            nc.scalar.activation(
+                out=y_rows[:],
+                in_=acc[:].rearrange("s (p t) -> s t p", t=PACK),
+                func=ACT.Copy,
+                scale=gate_col[:, e : e + 1],
+            )
+            turned = psum.tile([P, PACK, C2], F32, name="y_turned")
+            for t in range(PACK):
+                nc.tensor.transpose(turned[:, t, :], y_rows[:, t, :], ident[:])
+            nc.scalar.copy(out=y_sb[:, :, e * C2 : (e + 1) * C2], in_=turned[:])
+
+        def scatter(t, lo, hi):
+            nc.vector.tensor_copy(out_sb[t][:].indirect(entries(dst_sb, lo, hi)), y_sb[:, t, lo:hi])
+
+        first_level(0, [(0, P), (P, C1)])
+        first_level(1, [(0, C1)])
+        second_level(0)
+        second_level(1)
+        first_level(2, [(0, C1)])
+        for e in range(2, E):
+            second_level(e)
+        for e in range(EARLY):
+            for t in range(PACK):
+                scatter(t, e * C2, (e + 1) * C2)
+
+        out_rows = out_0.rearrange("(p t) c -> t p c", t=PACK)
+        out_bf_planes = out_bf[:].rearrange("p (c t) -> p c t", t=PACK)
+        chunk = 256
+        own = slice(0, chunk)
+        rest = slice(chunk, T)
+        last_two = keep.tile([P, 2, T - chunk], BF16, name="last_two", align_bytes=64)
+        for t in range(PACK):
+            scatter(t, EARLY * C2, T)
+            nc.sync.dma_start(out=out_rows[t], in_=out_sb[t][:])
+            if t < 2:
+                nc.scalar.copy(out=out_bf_planes[:, :, t], in_=out_sb[t][:])
+            else:
+                nc.scalar.copy(out=out_bf_planes[:, own, t], in_=out_sb[t][:, own])
+            if t == 2:
+                nc.scalar.copy(out=last_two[:, 0, :], in_=out_sb[t][:, rest])
+        nc.vector.tensor_copy(last_two[:, 1, :], out_sb[3][:, rest])
+        nc.vector.tensor_copy(out_bf_planes[:, rest, 2:4], last_two[:].rearrange("p t c -> p c t"))
+        out_1_words = words_of(out_1[0])
+        for cols in (own, rest):
+            nc.vector.quantize_mx(
+                out=out_codes[:, cols].bitcast(FP8X4),
+                scales=out_scales[:, cols],
+                in_=out_bf[:, PACK * cols.start : PACK * cols.stop],
+            )
+            nc.sync.dma_start(out=out_1_words[:, cols], in_=out_codes[:, cols])
+        for r in range(4):
+            queue = nc.sync if r % 2 else nc.scalar
+            queue.dma_start(out=out_2[0][r:16:4].bitcast(I32), in_=out_scales[r:P:32].bitcast(I32))

@@ -20,12 +20,12 @@ P = 128
 PACK = 4
 LIST = 16
 MIN_WINDOW = 512
-PAIR_BASE = (0, 3 * C1, 5 * C1)
+PAIR_AT = ((C1, 0), (3 * C1, 4 * C1))
 EARLY = 3
 
 
-def load_scale_rows(queue, plane, rows):
-    for r in range(4):
+def load_scale_rows(queue, plane, rows, which=range(4)):
+    for r in which:
         queue.dma_start(out=plane[r:P:32].bitcast(I32), in_=rows[r:16:4].bitcast(I32))
 
 
@@ -35,7 +35,7 @@ def tile_moe_hie_silu_kernel(
     nc = tc.nc
     with ExitStack() as ctx:
         keep = ctx.enter_context(tc.tile_pool(name="keep", bufs=1))
-        ring = ctx.enter_context(tc.tile_pool(name="ring", bufs=3))
+        ring = ctx.enter_context(tc.tile_pool(name="ring", bufs=4))
         psum = ctx.enter_context(tc.psum_pool(name="psum", bufs=2))
 
         offs_sb = keep.tile([P, T // LIST], U16, name="offs_sb")
@@ -49,7 +49,7 @@ def tile_moe_hie_silu_kernel(
         we_sb = [keep.tile([P, N], I32, name="we_sb%d" % e, align_bytes=64) for e in range(E)]
         gate_col = keep.tile([P, E], F32, name="gate_col")
         ident = keep.tile([P, P], F32, name="ident")
-        pairs = keep.tile([P, 7 * C1], F32, name="pairs", align_bytes=64)
+        pairs = keep.tile([P, 5 * C1], F32, name="pairs", align_bytes=64)
         y_sb = keep.tile([P, PACK, T], F32, name="y_sb", align_bytes=64)
         out_sb = [keep.tile([P, T], F32, name="out_sb%d" % t, align_bytes=64) for t in range(PACK)]
         out_bf = keep.tile([P, T * PACK], BF16, name="out_bf", align_bytes=64)
@@ -57,9 +57,11 @@ def tile_moe_hie_silu_kernel(
         out_scales = keep.tile([P, T], U8, name="out_scales", align_bytes=64)
 
         nc.gpsimd.memset(xs_sb[:].bitcast(I32), 0)
-        nc.gpsimd.memset(wgs_sb[:].bitcast(I32), 0)
         make_identity(nc, ident[:])
-        nc.vector.memset(wes_sb[:].bitcast(I32), 0)
+        ident_bf = keep.tile([P, P], BF16, name="ident_bf")
+        make_identity(nc, ident_bf[:])
+        planes = keep.tile([P, 6 * C1], BF16, name="planes", align_bytes=64)
+        nc.gpsimd.memset(planes[:, : 2 * C1], 0.0)
         nc.scalar.activation(
             out=pairs[:, 2 * C1 : 3 * C1].rearrange("p (a b) -> p a b", a=2),
             in_=ident[:].unsqueeze(1).to_broadcast([P, 2, P]),
@@ -70,11 +72,13 @@ def tile_moe_hie_silu_kernel(
         def words_of(ap):
             return ap.rearrange("p n d -> p (n d)").bitcast(I32)
 
-        nc.sync.dma_start(out=x_sb[:], in_=words_of(x_words[0]))
+        wg_scale_rows = wg_scales.rearrange("f s b i -> b (f s) i")
         nc.sync.dma_start(offs_sb[:], offs)
         load_scale_rows(nc.scalar, xs_sb, x_scales[0])
+        load_scale_rows(nc.sync, wgs_sb, wg_scale_rows, range(1))
+        nc.sync.dma_start(out=x_sb[:], in_=words_of(x_words[0]))
         nc.sync.dma_start(out=wg_sb[0][:].bitcast(I32), in_=wg_words[0, 0].bitcast(I32))
-        load_scale_rows(nc.sync, wgs_sb, wg_scales.rearrange("f s b i -> b (f s) i"))
+        load_scale_rows(nc.sync, wgs_sb, wg_scale_rows, range(1, 4))
         nc.sync.dma_start(out=wg_sb[1][:].bitcast(I32), in_=wg_words[1, 0].bitcast(I32))
         nc.sync.dma_start(offs2_sb[:], offs2)
         nc.sync.dma_start(out=wg_sb[2][:].bitcast(I32), in_=wg_words[2, 0].bitcast(I32))
@@ -89,14 +93,22 @@ def tile_moe_hie_silu_kernel(
         def entries(lst, lo, hi):
             return lst[:, lo // LIST : hi // LIST]
 
-        def first_level(f, cuts):
-            xg = keep.tile([P, C1], I32, name="xg%d" % f, align_bytes=64)
-            xgs = keep.tile([P, C1], U8, name="xgs%d" % f, align_bytes=64)
-            for lo, hi in cuts:
-                slots = entries(offs_sb, f * C1 + lo, f * C1 + hi)
-                nc.vector.tensor_copy(xg[:, lo:hi].bitcast(U32), x_sb[:].bitcast(U32).indirect(slots))
-                nc.vector.tensor_copy(xgs[:, lo:hi], xs_sb[:].indirect(slots))
-            turned = psum.tile([P, 2, C1], F32, name="a_turned")
+        def gather_tokens(f0, f1):
+            n = (f1 - f0) * C1
+            xg = keep.tile([P, n], I32, name="xg%d" % f0, align_bytes=64)
+            xgs = keep.tile([P, n], U8, name="xgs%d" % f0, align_bytes=64)
+            step = P if f0 == 0 else n
+            for lo in range(0, n, step):
+                slots = entries(offs_sb, f0 * C1 + lo, f0 * C1 + lo + step)
+                nc.vector.tensor_copy(xg[:, lo : lo + step].bitcast(U32), x_sb[:].bitcast(U32).indirect(slots))
+                nc.vector.tensor_copy(xgs[:, lo : lo + step], xs_sb[:].indirect(slots))
+            return [(xg[:, j * C1 : (j + 1) * C1], xgs[:, j * C1 : (j + 1) * C1]) for j in range(f1 - f0)]
+
+        def first_level(f, xg, xgs):
+            by_pairs = f < G - 1
+            d = 2 if by_pairs else 1
+            parts = [(0, 1), (1, 2)] if f == 0 else [(0, PACK // d)]
+            accs, rows = [], []
             for h in range(C1 // P):
                 cols = slice(h * P, (h + 1) * P)
                 acc = psum.tile([P, H], F32, name="a_acc")
@@ -109,90 +121,129 @@ def tile_moe_hie_silu_kernel(
                     start=True,
                     stop=True,
                 )
-                a_rows = ring.tile([P, H], BF16, name="a_rows", align_bytes=64)
-                nc.scalar.activation(
-                    out=a_rows[:].rearrange("s (u p d) -> s u p d", u=2, d=2),
-                    in_=acc[:].rearrange("s (p u d) -> s u p d", u=2, d=2),
-                    func=ACT.Silu,
-                )
-                a_words = a_rows[:].bitcast(F32)
+                accs.append(acc)
+                rows.append(ring.tile([P, H], BF16, name="a_rows", align_bytes=64))
+            turned = [
+                psum.tile([P, u1 - u0, C1], F32 if by_pairs else BF16, name="a_turned") for u0, u1 in parts
+            ]
+            for h in range(C1 // P):
+                elems = rows[h][:].bitcast(F32) if by_pairs else rows[h][:]
+                for u0, u1 in parts if h == 1 else [(0, PACK // d)]:
+                    nc.scalar.activation(
+                        out=rows[h][:].rearrange("s (u p d) -> s u p d", p=P, d=d)[:, u0:u1],
+                        in_=accs[h][:].rearrange("s (p u d) -> s u p d", p=P, d=d)[:, u0:u1],
+                        func=ACT.Silu,
+                    )
+                for bank, (u0, u1) in zip(turned, parts):
+                    for u in range(u0, u1):
+                        nc.tensor.transpose(
+                            bank[:, u - u0, h * P : (h + 1) * P],
+                            elems[:, u * P : (u + 1) * P],
+                            (ident if by_pairs else ident_bf)[:],
+                        )
+            for bank, (u0, u1) in zip(turned, parts):
+                width = (u1 - u0) * C1
+                base = PAIR_AT[f][u0] if by_pairs else 2 * C1
+                target = (pairs if by_pairs else planes)[:, base : base + width]
+                move = nc.vector.tensor_copy if (f, u0) == (0, 1) else nc.scalar.copy
+                move(out=target, in_=bank[:].rearrange("p u s -> p (u s)"))
+
+        quantised = {}
+
+        def gather_and_quantise(e0, e1):
+            f = e0 // 2
+            n = (e1 - e0) * C2
+            slots = entries(offs2_sb, e0 * C2, e1 * C2)
+            ag = keep.tile([P, n * PACK], BF16, name="ag%d" % e0, align_bytes=64)
+            if f == G - 1:
+                ag_planes = ag[:].rearrange("p (s t) -> p s t", t=PACK)
+                for t in range(PACK):
+                    window = planes[:, t * C1 : t * C1 + T]
+                    nc.scalar.activation(ag_planes[:, :, t], window.indirect(slots), ACT.Copy)
+            else:
+                ag_words = ag[:].bitcast(U32).rearrange("p (s u) -> p s u", u=2)
                 for u in range(2):
-                    nc.tensor.transpose(turned[:, u, cols], a_words[:, u * P : (u + 1) * P], ident[:])
-            base = PAIR_BASE[f]
-            nc.scalar.copy(out=pairs[:, base : base + 2 * C1], in_=turned[:].rearrange("p u s -> p (u s)"))
+                    start = PAIR_AT[f][u] - f * C1
+                    window = pairs[:, start : start + MIN_WINDOW].bitcast(U32)
+                    nc.vector.tensor_copy(ag_words[:, :, u], window.indirect(slots))
+            aq = keep.tile([P, n], I32, name="aq%d" % e0, align_bytes=64)
+            aqs = keep.tile([P, n], U8, name="aqs%d" % e0, align_bytes=64)
+            nc.vector.quantize_mx(out=aq[:].bitcast(FP8X4), scales=aqs[:], in_=ag[:])
+            for e in range(e0, e1):
+                cols = slice((e - e0) * C2, (e - e0 + 1) * C2)
+                quantised[e] = (aq[:, cols], aqs[:, cols])
 
         def second_level(e):
-            f = e // 2
-            slots = entries(offs2_sb, e * C2, (e + 1) * C2)
-            ag = ring.tile([P, C2 * PACK], BF16, name="ag", align_bytes=64)
-            ag_words = ag[:].bitcast(U32).rearrange("p (s u) -> p s u", u=2)
-            ag_halves = ring.tile([P, 2, C2], I32, name="ag_halves", align_bytes=64)
-            width = max(MIN_WINDOW, (f + 1) * C1)
-            for u in range(2):
-                start = PAIR_BASE[f] + (u - f) * C1
-                window = pairs[:, start : start + width].bitcast(U32)
-                target = ag_words[:, :, u] if e == 0 else ag_halves[:, u, :].bitcast(U32)
-                nc.vector.tensor_copy(target, window.indirect(slots))
-            if e > 0:
-                nc.scalar.copy(out=ag_words, in_=ag_halves[:].bitcast(U32).rearrange("p u s -> p s u"))
-            aq = ring.tile([P, C2], I32, name="aq", align_bytes=64)
-            aqs = ring.tile([P, C2], U8, name="aqs", align_bytes=64)
-            nc.vector.quantize_mx(out=aq[:].bitcast(FP8X4), scales=aqs[:], in_=ag[:])
+            aq, aqs = quantised[e]
             acc = psum.tile([P, N], F32, name="y_acc")
             nc.tensor.matmul_mx(
                 out=acc[:],
-                lhsT=aq[:].bitcast(FP8X4),
-                lhsT_scale=aqs[:],
+                lhsT=aq.bitcast(FP8X4),
+                lhsT_scale=aqs,
                 rhs=we_sb[e][:].bitcast(FP8X4),
                 rhs_scale=wes_sb[:, e, :],
                 start=True,
                 stop=True,
             )
             y_rows = ring.tile([P, PACK, P], F32, name="y_rows", align_bytes=64)
-            nc.scalar.activation(
-                out=y_rows[:],
-                in_=acc[:].rearrange("s (p t) -> s t p", t=PACK),
-                func=ACT.Copy,
-                scale=gate_col[:, e : e + 1],
-            )
-            turned = psum.tile([P, PACK, C2], F32, name="y_turned")
-            for t in range(PACK):
-                nc.tensor.transpose(turned[:, t, :], y_rows[:, t, :], ident[:])
-            nc.scalar.copy(out=y_sb[:, :, e * C2 : (e + 1) * C2], in_=turned[:])
+            for t0, t1 in [(0, 2), (2, PACK)] if e == 0 else [(0, PACK)]:
+                nc.scalar.activation(
+                    out=y_rows[:, t0:t1],
+                    in_=acc[:].rearrange("s (p t) -> s t p", t=PACK)[:, t0:t1],
+                    func=ACT.Copy,
+                    scale=gate_col[:, e : e + 1],
+                )
+                turned = psum.tile([P, t1 - t0, C2], F32, name="y_turned")
+                for t in range(t0, t1):
+                    nc.tensor.transpose(turned[:, t - t0, :], y_rows[:, t, :], ident[:])
+                nc.scalar.copy(out=y_sb[:, t0:t1, e * C2 : (e + 1) * C2], in_=turned[:])
 
         def scatter(t, lo, hi):
             nc.vector.tensor_copy(out_sb[t][:].indirect(entries(dst_sb, lo, hi)), y_sb[:, t, lo:hi])
 
-        first_level(0, [(0, P), (P, C1)])
-        first_level(1, [(0, C1)])
-        second_level(0)
-        second_level(1)
-        first_level(2, [(0, C1)])
-        for e in range(2, E):
-            second_level(e)
-        for e in range(EARLY):
+        def scatter_expert(e):
             for t in range(PACK):
                 scatter(t, e * C2, (e + 1) * C2)
+
+        tokens = gather_tokens(0, 1) + gather_tokens(1, G)
+        first_level(0, *tokens[0])
+        gather_and_quantise(0, 1)
+        second_level(0)
+        first_level(1, *tokens[1])
+        gather_and_quantise(1, 2)
+        gather_and_quantise(2, 4)
+        first_level(2, *tokens[2])
+        scatter_expert(0)
+        gather_and_quantise(4, 5)
+        second_level(1)
+        scatter_expert(1)
+        gather_and_quantise(5, 6)
+        second_level(2)
+        scatter_expert(2)
+        for e in range(EARLY, E):
+            second_level(e)
 
         out_rows = out_0.rearrange("(p t) c -> t p c", t=PACK)
         out_bf_planes = out_bf[:].rearrange("p (c t) -> p c t", t=PACK)
         chunk = 256
-        own = slice(0, chunk)
-        rest = slice(chunk, T)
-        last_two = keep.tile([P, 2, T - chunk], BF16, name="last_two", align_bytes=64)
+        own = slice(0, T // 2)
+        rest = slice(T // 2, T)
+        last_two = keep.tile([P, 2, T // 2], BF16, name="last_two", align_bytes=64)
         for t in range(PACK):
             scatter(t, EARLY * C2, T)
             nc.sync.dma_start(out=out_rows[t], in_=out_sb[t][:])
             if t < 2:
                 nc.scalar.copy(out=out_bf_planes[:, :, t], in_=out_sb[t][:])
             else:
-                nc.scalar.copy(out=out_bf_planes[:, own, t], in_=out_sb[t][:, own])
+                for cols in (slice(0, chunk), slice(chunk, own.stop)):
+                    nc.scalar.copy(out=out_bf_planes[:, cols, t], in_=out_sb[t][:, cols])
             if t == 2:
                 nc.scalar.copy(out=last_two[:, 0, :], in_=out_sb[t][:, rest])
         nc.vector.tensor_copy(last_two[:, 1, :], out_sb[3][:, rest])
         nc.vector.tensor_copy(out_bf_planes[:, rest, 2:4], last_two[:].rearrange("p t c -> p c t"))
         out_1_words = words_of(out_1[0])
-        for cols in (own, rest):
+        for c in (0, 2, 1):
+            cols = slice(c * chunk, (c + 1) * chunk)
             nc.vector.quantize_mx(
                 out=out_codes[:, cols].bitcast(FP8X4),
                 scales=out_scales[:, cols],

from contextlib import ExitStack

import concourse.mybir as mybir
from concourse.masks import make_identity

K, T, G, C1, E, C2, H, N = 512, 768, 3, 256, 6, 128, 512, 512
FLOPS = 2 * T * K * H + 2 * T * H * N

F32 = mybir.dt.float32
BF16 = mybir.dt.bfloat16
I32 = mybir.dt.int32
U32 = mybir.dt.uint32
U16 = mybir.dt.uint16
U8 = mybir.dt.uint8
FP8X4 = mybir.dt.float8_e4m3fn_x4
FP4X4 = mybir.dt.float4_e2m1fn_x4
ACT = mybir.ActivationFunctionType

P = 128
PACK = 4
LIST = 16
MIN_WINDOW = 512
PAIR_AT = ((C1, 0), (3 * C1, 4 * C1))
EARLY = 3


def load_scale_rows(queue, plane, rows, which=range(4)):
    for r in which:
        queue.dma_start(out=plane[r:P:32].bitcast(I32), in_=rows[r:16:4].bitcast(I32))


def tile_moe_hie_silu_kernel(
    tc, x_words, x_scales, wg_words, wg_scales, we_words, we_scales, gate, offs, offs2, dst, out_0, out_1, out_2
):
    nc = tc.nc
    with ExitStack() as ctx:
        keep = ctx.enter_context(tc.tile_pool(name="keep", bufs=1))
        ring = ctx.enter_context(tc.tile_pool(name="ring", bufs=4))
        psum = ctx.enter_context(tc.psum_pool(name="psum", bufs=2))

        offs_sb = keep.tile([P, T // LIST], U16, name="offs_sb")
        offs2_sb = keep.tile([P, T // LIST], U16, name="offs2_sb")
        dst_sb = keep.tile([P, T // LIST], U16, name="dst_sb")
        x_sb = keep.tile([P, T], I32, name="x_sb", align_bytes=64)
        xs_sb = keep.tile([P, T], U8, name="xs_sb", align_bytes=64)
        wgs_sb = keep.tile([P, G, H], U8, name="wgs_sb", align_bytes=64)
        wes_sb = keep.tile([P, E, N], U8, name="wes_sb", align_bytes=64)
        wg_sb = [keep.tile([P, 2 * H], U8, name="wg_sb%d" % f, align_bytes=64) for f in range(G)]
        we_sb = [keep.tile([P, N], I32, name="we_sb%d" % e, align_bytes=64) for e in range(E)]
        gate_col = keep.tile([P, E], F32, name="gate_col")
        ident = keep.tile([P, P], F32, name="ident")
        pairs = keep.tile([P, 5 * C1], F32, name="pairs", align_bytes=64)
        y_sb = keep.tile([P, PACK, T], F32, name="y_sb", align_bytes=64)
        out_sb = [keep.tile([P, T], F32, name="out_sb%d" % t, align_bytes=64) for t in range(PACK)]
        out_bf = keep.tile([P, T * PACK], BF16, name="out_bf", align_bytes=64)
        out_codes = keep.tile([P, T], I32, name="out_codes", align_bytes=64)
        out_scales = keep.tile([P, T], U8, name="out_scales", align_bytes=64)

        nc.gpsimd.memset(xs_sb[:].bitcast(I32), 0)
        make_identity(nc, ident[:])
        ident_bf = keep.tile([P, P], BF16, name="ident_bf")
        make_identity(nc, ident_bf[:])
        planes = keep.tile([P, 6 * C1], BF16, name="planes", align_bytes=64)
        nc.gpsimd.memset(planes[:, : 2 * C1], 0.0)
        nc.scalar.activation(
            out=pairs[:, 2 * C1 : 3 * C1].rearrange("p (a b) -> p a b", a=2),
            in_=ident[:].unsqueeze(1).to_broadcast([P, 2, P]),
            func=ACT.Silu,
            scale=0.0,
        )

        def words_of(ap):
            return ap.rearrange("p n d -> p (n d)").bitcast(I32)

        wg_scale_rows = wg_scales.rearrange("f s b i -> b (f s) i")
        nc.sync.dma_start(offs_sb[:], offs)
        load_scale_rows(nc.scalar, xs_sb, x_scales[0])
        load_scale_rows(nc.sync, wgs_sb, wg_scale_rows, range(1))
        nc.sync.dma_start(out=x_sb[:], in_=words_of(x_words[0]))
        nc.sync.dma_start(out=wg_sb[0][:].bitcast(I32), in_=wg_words[0, 0].bitcast(I32))
        load_scale_rows(nc.sync, wgs_sb, wg_scale_rows, range(1, 4))
        nc.sync.dma_start(out=wg_sb[1][:].bitcast(I32), in_=wg_words[1, 0].bitcast(I32))
        nc.sync.dma_start(offs2_sb[:], offs2)
        nc.sync.dma_start(out=wg_sb[2][:].bitcast(I32), in_=wg_words[2, 0].bitcast(I32))
        nc.sync.dma_start(out=we_sb[0][:], in_=words_of(we_words[0, 0]))
        load_scale_rows(nc.sync, wes_sb, we_scales.rearrange("e s b n -> b (e s) n"))
        with nc.allow_non_contiguous_dma(reason="one gate value a partition and expert"):
            nc.sync.dma_start(out=gate_col[:], in_=gate[0].rearrange("(e m) -> m e", m=C2))
        nc.sync.dma_start(dst_sb[:], dst)
        for e in range(1, E):
            nc.sync.dma_start(out=we_sb[e][:], in_=words_of(we_words[e, 0]))

        def entries(lst, lo, hi):
            return lst[:, lo // LIST : hi // LIST]

        def gather_tokens(f0, f1):
            n = (f1 - f0) * C1
            xg = keep.tile([P, n], I32, name="xg%d" % f0, align_bytes=64)
            xgs = keep.tile([P, n], U8, name="xgs%d" % f0, align_bytes=64)
            step = P if f0 == 0 else n
            for lo in range(0, n, step):
                slots = entries(offs_sb, f0 * C1 + lo, f0 * C1 + lo + step)
                nc.vector.tensor_copy(xg[:, lo : lo + step].bitcast(U32), x_sb[:].bitcast(U32).indirect(slots))
                nc.vector.tensor_copy(xgs[:, lo : lo + step], xs_sb[:].indirect(slots))
            return [(xg[:, j * C1 : (j + 1) * C1], xgs[:, j * C1 : (j + 1) * C1]) for j in range(f1 - f0)]

        def first_level(f, xg, xgs):
            by_pairs = f < G - 1
            d = 2 if by_pairs else 1
            parts = [(0, 1), (1, 2)] if f == 0 else [(0, PACK // d)]
            accs, rows = [], []
            for h in range(C1 // P):
                cols = slice(h * P, (h + 1) * P)
                acc = psum.tile([P, H], F32, name="a_acc")
                nc.tensor.matmul_mx(
                    out=acc[:],
                    lhsT=xg[:, cols].bitcast(FP8X4),
                    lhsT_scale=xgs[:, cols],
                    rhs=wg_sb[f][:].bitcast(FP4X4),
                    rhs_scale=wgs_sb[:, f, :],
                    start=True,
                    stop=True,
                )
                accs.append(acc)
                rows.append(ring.tile([P, H], BF16, name="a_rows", align_bytes=64))
            turned = [
                psum.tile([P, u1 - u0, C1], F32 if by_pairs else BF16, name="a_turned") for u0, u1 in parts
            ]
            for h in range(C1 // P):
                elems = rows[h][:].bitcast(F32) if by_pairs else rows[h][:]
                for u0, u1 in parts if h == 1 else [(0, PACK // d)]:
                    nc.scalar.activation(
                        out=rows[h][:].rearrange("s (u p d) -> s u p d", p=P, d=d)[:, u0:u1],
                        in_=accs[h][:].rearrange("s (p u d) -> s u p d", p=P, d=d)[:, u0:u1],
                        func=ACT.Silu,
                    )
                for bank, (u0, u1) in zip(turned, parts):
                    for u in range(u0, u1):
                        nc.tensor.transpose(
                            bank[:, u - u0, h * P : (h + 1) * P],
                            elems[:, u * P : (u + 1) * P],
                            (ident if by_pairs else ident_bf)[:],
                        )
            for bank, (u0, u1) in zip(turned, parts):
                width = (u1 - u0) * C1
                base = PAIR_AT[f][u0] if by_pairs else 2 * C1
                target = (pairs if by_pairs else planes)[:, base : base + width]
                move = nc.vector.tensor_copy if (f, u0) == (0, 1) else nc.scalar.copy
                move(out=target, in_=bank[:].rearrange("p u s -> p (u s)"))

        quantised = {}

        def gather_and_quantise(e0, e1):
            f = e0 // 2
            n = (e1 - e0) * C2
            slots = entries(offs2_sb, e0 * C2, e1 * C2)
            ag = keep.tile([P, n * PACK], BF16, name="ag%d" % e0, align_bytes=64)
            if f == G - 1:
                ag_planes = ag[:].rearrange("p (s t) -> p s t", t=PACK)
                for t in range(PACK):
                    window = planes[:, t * C1 : t * C1 + T]
                    nc.scalar.activation(ag_planes[:, :, t], window.indirect(slots), ACT.Copy)
            else:
                ag_words = ag[:].bitcast(U32).rearrange("p (s u) -> p s u", u=2)
                for u in range(2):
                    start = PAIR_AT[f][u] - f * C1
                    window = pairs[:, start : start + MIN_WINDOW].bitcast(U32)
                    nc.vector.tensor_copy(ag_words[:, :, u], window.indirect(slots))
            aq = keep.tile([P, n], I32, name="aq%d" % e0, align_bytes=64)
            aqs = keep.tile([P, n], U8, name="aqs%d" % e0, align_bytes=64)
            nc.vector.quantize_mx(out=aq[:].bitcast(FP8X4), scales=aqs[:], in_=ag[:])
            for e in range(e0, e1):
                cols = slice((e - e0) * C2, (e - e0 + 1) * C2)
                quantised[e] = (aq[:, cols], aqs[:, cols])

        def second_level(e):
            aq, aqs = quantised[e]
            acc = psum.tile([P, N], F32, name="y_acc")
            nc.tensor.matmul_mx(
                out=acc[:],
                lhsT=aq.bitcast(FP8X4),
                lhsT_scale=aqs,
                rhs=we_sb[e][:].bitcast(FP8X4),
                rhs_scale=wes_sb[:, e, :],
                start=True,
                stop=True,
            )
            y_rows = ring.tile([P, PACK, P], F32, name="y_rows", align_bytes=64)
            for t0, t1 in [(0, 2), (2, PACK)] if e == 0 else [(0, PACK)]:
                nc.scalar.activation(
                    out=y_rows[:, t0:t1],
                    in_=acc[:].rearrange("s (p t) -> s t p", t=PACK)[:, t0:t1],
                    func=ACT.Copy,
                    scale=gate_col[:, e : e + 1],
                )
                turned = psum.tile([P, t1 - t0, C2], F32, name="y_turned")
                for t in range(t0, t1):
                    nc.tensor.transpose(turned[:, t - t0, :], y_rows[:, t, :], ident[:])
                nc.scalar.copy(out=y_sb[:, t0:t1, e * C2 : (e + 1) * C2], in_=turned[:])

        def scatter(t, lo, hi):
            nc.vector.tensor_copy(out_sb[t][:].indirect(entries(dst_sb, lo, hi)), y_sb[:, t, lo:hi])

        def scatter_expert(e):
            for t in range(PACK):
                scatter(t, e * C2, (e + 1) * C2)

        tokens = gather_tokens(0, 1) + gather_tokens(1, G)
        first_level(0, *tokens[0])
        gather_and_quantise(0, 1)
        second_level(0)
        first_level(1, *tokens[1])
        gather_and_quantise(1, 2)
        gather_and_quantise(2, 4)
        first_level(2, *tokens[2])
        scatter_expert(0)
        gather_and_quantise(4, 5)
        second_level(1)
        scatter_expert(1)
        gather_and_quantise(5, 6)
        second_level(2)
        scatter_expert(2)
        for e in range(EARLY, E):
            second_level(e)

        out_rows = out_0.rearrange("(p t) c -> t p c", t=PACK)
        out_bf_planes = out_bf[:].rearrange("p (c t) -> p c t", t=PACK)
        chunk = 256
        own = slice(0, T // 2)
        rest = slice(T // 2, T)
        last_two = keep.tile([P, 2, T // 2], BF16, name="last_two", align_bytes=64)
        for t in range(PACK):
            scatter(t, EARLY * C2, T)
            nc.sync.dma_start(out=out_rows[t], in_=out_sb[t][:])
            if t < 2:
                nc.scalar.copy(out=out_bf_planes[:, :, t], in_=out_sb[t][:])
            else:
                for cols in (slice(0, chunk), slice(chunk, own.stop)):
                    nc.scalar.copy(out=out_bf_planes[:, cols, t], in_=out_sb[t][:, cols])
            if t == 2:
                nc.scalar.copy(out=last_two[:, 0, :], in_=out_sb[t][:, rest])
        nc.vector.tensor_copy(last_two[:, 1, :], out_sb[3][:, rest])
        nc.vector.tensor_copy(out_bf_planes[:, rest, 2:4], last_two[:].rearrange("p t c -> p c t"))
        out_1_words = words_of(out_1[0])
        for c in (0, 2, 1):
            cols = slice(c * chunk, (c + 1) * chunk)
            nc.vector.quantize_mx(
                out=out_codes[:, cols].bitcast(FP8X4),
                scales=out_scales[:, cols],
                in_=out_bf[:, PACK * cols.start : PACK * cols.stop],
            )
            nc.sync.dma_start(out=out_1_words[:, cols], in_=out_codes[:, cols])
        for r in range(4):
            queue = nc.sync if r % 2 else nc.scalar
            queue.dma_start(out=out_2[0][r:16:4].bitcast(I32), in_=out_scales[r:P:32].bitcast(I32))
